import numpy as np
import ml_dtypes


def mxq(x, axis, fmt="e4m3"):
    dtype, down = {"e4m3": (ml_dtypes.float8_e4m3fn, 7), "e5m2": (ml_dtypes.float8_e5m2, 14)}[fmt]
    v = np.moveaxis(np.asarray(x, np.float32).astype(ml_dtypes.bfloat16).astype(np.float64), axis, -1)
    blocks = v.reshape(v.shape[:-1] + (-1, 32))
    amax = np.abs(blocks).max(-1, keepdims=True)
    byte = np.maximum(np.where(amax > 0, np.frexp(amax)[1] - 1 + 127, 0) - down, 1)
    scale = np.exp2(byte - 127.0)
    codes = (blocks / scale).astype(np.float32).astype(dtype).astype(np.float64)
    return np.moveaxis((codes * scale).reshape(v.shape), -1, axis)


WIDE = False


def mx_kscale(k, group=512):
    if not WIDE:
        return np.ones(k)
    levels = np.array([18, -18])
    if group != 512:
        return np.exp2(np.random.permutation(np.resize(levels, k // group))).repeat(group)
    if k % 512:
        return np.exp2(np.random.permutation(np.resize(levels, k // 32))).repeat(32)
    a = np.empty((k // 512, 16))
    for p in range(k // 512):
        a[p, :8] = np.random.permutation(np.resize(levels, 8))
        for g in range(8):
            far = levels[np.abs(levels - a[p, g]) >= 10]
            a[p, g + 8] = far[np.random.randint(len(far))]
    return np.exp2(a.ravel()).repeat(32)


def f64(x):
    return np.asarray(x).astype(np.float64)


H, D, N = 4, 128, 1024


def setup_inputs():
    n = np.random.standard_normal
    s = mx_kscale(D, 0)
    u = mx_kscale(N)
    t = np.random.uniform(0.5, 2.0, N) * u
    v = n((H, N, 128))
    return {
        "q": n((H, D, N)).astype(np.float32),
        "qa": (np.random.uniform(0.5, 2.0, D) * s)[:, None].astype(np.float32),
        "ka": np.tile(np.random.uniform(0.5, 2.0, D) / s, (128, 1)).astype(np.float32),
        "k": n((H, N, D)).astype(np.float32),
        "t": t.reshape(N, 1).astype(np.float32),
        "v": (v / t[:, None]).astype(np.float32),
        "og": n((H, N, 128)).astype(np.float32),
    }


def reference(q, qa, ka, k, t, v, og):
    fq = (1.0 / (1.0 + np.exp(-f64(q)))) * f64(qa)
    fk = (1.0 / (1.0 + np.exp(-f64(k)))) * f64(t) * f64(ka)[:1]
    S = (mxq(fk, 1, "e4m3").transpose(0, 2, 1) @ mxq(f64(v), 1, "e4m3")) / N
    y = mxq(fq, 1, "e4m3").transpose(0, 2, 1) @ mxq(S, 1, "e4m3")
    y = y / (1.0 + np.exp(-f64(og)))
    return y

@@ -1,0 +1,232 @@
+from contextlib import ExitStack
+
+import concourse.mybir as mybir
+
+H, D, N = 4, 128, 1024
+FLOPS = 2 * 2 * H * N * D * D
+
+F32 = mybir.dt.float32
+BF16 = mybir.dt.bfloat16
+U32 = mybir.dt.uint32
+U8 = mybir.dt.uint8
+FP8X4 = mybir.dt.float8_e4m3fn_x4
+SIGMOID = mybir.ActivationFunctionType.Sigmoid
+COPY = mybir.ActivationFunctionType.Copy
+MULT = mybir.AluOpType.mult
+
+P = 128
+PACK = 4
+ROWS = D // PACK
+PASSES = N // (P * PACK)
+TILES = N // P
+HALVES = 2
+BANK_TILES = 4
+
+
+def tile_rows_lin_sig_gate_kernel(tc, q, qa, ka, k, t, v, og, out):
+    nc = tc.nc
+    with ExitStack() as ctx:
+        sb = ctx.enter_context(tc.tile_pool(name="sb", bufs=1))
+        ps = ctx.enter_context(tc.psum_pool(name="ps", bufs=1))
+        ctx.enter_context(tc.manual_schedule())
+
+        def sbuf(name, shape, dtype):
+            return sb.tile(shape, dtype, name=name, align_bytes=64)
+
+        ka_sb = sbuf("ka", [P, D], F32)
+        t_sb = sbuf("t", [P, PASSES, PACK], F32)
+        qa_sb = sbuf("qa", [P, PACK], F32)
+        k_raw = [[sbuf("k_raw%d%d" % (g, h), [P, PACK, D], F32) for h in range(H)] for g in range(PASSES)]
+        q_raw = [[sbuf("q_raw%d%d" % (a, u), [P, 2, N // HALVES], F32) for u in range(2)] for a in range(HALVES)]
+        v_raw = [sbuf("v_raw%d" % h, [P, PASSES, PACK, D], F32) for h in range(H)]
+        og_raw = [sbuf("og_raw%d" % h, [P, TILES * D], F32) for h in range(H)]
+
+        nc.sync.dma_start(out=ka_sb[:], in_=ka)
+        nc.sync.dma_start(out=t_sb[:], in_=t.rearrange("(g p j) o -> p g (j o)", p=P, j=PACK))
+        for g in range(PASSES):
+            for h in range(H):
+                nc.sync.dma_start(out=k_raw[g][h][:], in_=k[h].rearrange("(g p j) d -> g p j d", p=P, j=PACK)[g])
+        nc.sync.dma_start(
+            out=qa_sb[:], in_=qa.rearrange("(p j) o -> p (j o)", j=PACK).unsqueeze(0).to_broadcast([H, ROWS, PACK])
+        )
+        q_rows = q.rearrange("h (p j) n -> (h p) j n", j=PACK)
+        for a in range(HALVES):
+            for u in range(2):
+                nc.sync.dma_start(out=q_raw[a][u][:], in_=q_rows[:, 2 * u : 2 * u + 2, 512 * a : 512 * (a + 1)])
+        for h in range(H):
+            nc.sync.dma_start(out=v_raw[h][:], in_=v[h].rearrange("(g p j) e -> p g j e", p=P, j=PACK))
+        for h in range(H):
+            nc.sync.dma_start(out=og_raw[h][:], in_=og[h].rearrange("(p r) e -> p (r e)", r=TILES))
+
+        tka = [sbuf("tka%d" % g, [P, PACK, ROWS, PACK], F32) for g in range(PASSES)]
+        k_sig = [[sbuf("k_sig%d%d" % (g, h), [P, PACK, ROWS, PACK], F32) for h in range(H)] for g in range(PASSES)]
+        fk = [sbuf("fk%d" % g, [P, PACK, H, ROWS * PACK], BF16) for g in range(PASSES)]
+        k_codes = [sbuf("k_codes%d" % g, [P, PACK * P], U32) for g in range(PASSES)]
+        k_scales = [sbuf("k_scales%d" % g, [P, PACK * P], U8) for g in range(PASSES)]
+        q_sig = [sbuf("q_sig%d" % a, [P, 2, N // HALVES, 2], F32) for a in range(HALVES)]
+        fq = [sbuf("fq%d" % b, [P, BANK_TILES, P, PACK], BF16) for b in range(2)]
+        q_codes = [sbuf("q_codes%d" % b, [P, BANK_TILES * P], U32) for b in range(2)]
+        q_scales = [sbuf("q_scales%d" % b, [P, BANK_TILES * P], U8) for b in range(2)]
+        vb = [sbuf("vb%d" % h, [P, PASSES, D, PACK], BF16) for h in range(H)]
+        v_codes = [sbuf("v_codes%d" % h, [P, PASSES * D], U32) for h in range(H)]
+        v_scales = [sbuf("v_scales%d" % h, [P, PASSES * D], U8) for h in range(H)]
+        state = sbuf("state", [P, D, PACK], BF16)
+        s_codes = sbuf("s_codes", [P, D], U32)
+        s_scales = sbuf("s_scales", [P, D], U8)
+        gate = [sbuf("gate%d" % h, [P, TILES * D], F32) for h in range(H)]
+        res = [sbuf("res%d" % h, [P, TILES * D], F32) for h in range(H)]
+        s_bank = [ps.tile([P, PACK, D], F32, name="s_bank%d" % h) for h in range(H)]
+        y_bank = [ps.tile([P, BANK_TILES * D], F32, name="y_bank%d" % h) for h in range(H)]
+
+        def quantize(codes, scales, values):
+            nc.vector.quantize_mx(out=codes[:].bitcast(FP8X4), scales=scales[:], in_=values)
+
+        def key_factors(g):
+            shape = [P, PACK, ROWS, PACK]
+            nc.vector.tensor_tensor(
+                out=tka[g][:],
+                in0=ka_sb[:].rearrange("p (c x) -> p x c", x=PACK).unsqueeze(3).to_broadcast(shape),
+                in1=t_sb[:, g, :].unsqueeze(1).unsqueeze(1).to_broadcast(shape),
+                op=MULT,
+            )
+
+        def key_sigmoid(g, h):
+            nc.scalar.activation(
+                out=k_sig[g][h][:].rearrange("p x c j -> p c j x"),
+                in_=k_raw[g][h][:].rearrange("p j (c x) -> p c j x", x=PACK),
+                func=SIGMOID,
+            )
+
+        def key_scale(g, h):
+            nc.vector.tensor_tensor(
+                out=fk[g][:, :, h, :],
+                in0=k_sig[g][h][:].rearrange("p x c j -> p x (c j)"),
+                in1=tka[g][:].rearrange("p x c j -> p x (c j)"),
+                op=MULT,
+            )
+
+        def key_quantize(g):
+            quantize(k_codes[g], k_scales[g], fk[g][:].rearrange("p x h w -> p (x h w)"))
+
+        def query_sigmoid(a, u):
+            nc.scalar.activation(out=q_sig[a][:, u, :, :], in_=q_raw[a][u][:].rearrange("p e n -> p n e"), func=SIGMOID)
+
+        def query_scale(a, r):
+            width = P // HALVES
+            shape = [P, width, 2, 2]
+            nc.vector.tensor_tensor(
+                out=fq[r // BANK_TILES][:, r % BANK_TILES, width * a : width * (a + 1), :].rearrange(
+                    "p s (u e) -> p s u e", u=2
+                ),
+                in0=q_sig[a][:].rearrange("p u (s r) e -> p r s u e", r=TILES)[:, r],
+                in1=qa_sb[:].rearrange("p (u e) -> p u e", u=2).unsqueeze(1).to_broadcast(shape),
+                op=MULT,
+            )
+
+        def query_quantize(b):
+            quantize(q_codes[b], q_scales[b], fq[b][:].rearrange("p r s j -> p (r s j)"))
+
+        def value_round(h, copy):
+            copy(
+                out=vb[h][:].rearrange("p g (c i) j -> p g c j i", i=4),
+                in_=v_raw[h][:].rearrange("p g j (c i) -> p g c j i", i=4),
+            )
+
+        def value_quantize(h):
+            quantize(v_codes[h], v_scales[h], vb[h][:].rearrange("p g e j -> p (g e j)"))
+
+        def state_products(h):
+            for x in range(PACK):
+                for g in range(PASSES):
+                    k_cols = slice(P * x, P * (x + 1))
+                    v_cols = slice(D * g, D * (g + 1))
+                    nc.tensor.matmul_mx(
+                        out=s_bank[h][:, x, :],
+                        lhsT=k_codes[g][:, k_cols].bitcast(FP8X4),
+                        lhsT_scale=k_scales[g][:, k_cols],
+                        rhs=v_codes[h][:, v_cols].bitcast(FP8X4),
+                        rhs_scale=v_scales[h][:, v_cols],
+                        start=(g == 0),
+                        stop=(g == PASSES - 1),
+                    )
+
+        def state_round(h):
+            rows = slice(ROWS * h, ROWS * (h + 1))
+            nc.scalar.activation(
+                out=state[rows, :, :], in_=s_bank[h][rows, :, :].rearrange("p x e -> p e x"), func=COPY, scale=1.0 / N
+            )
+
+        def read_state(h, b):
+            rows = slice(ROWS * h, ROWS * (h + 1))
+            for i in range(BANK_TILES):
+                cols = slice(P * i, P * (i + 1))
+                nc.tensor.matmul_mx(
+                    out=y_bank[h][:, cols],
+                    lhsT=q_codes[b][rows, cols].bitcast(FP8X4),
+                    lhsT_scale=q_scales[b][rows, cols],
+                    rhs=s_codes[rows, :].bitcast(FP8X4),
+                    rhs_scale=s_scales[rows, :],
+                    start=True,
+                    stop=True,
+                )
+
+        def gate_sigmoid(h):
+            nc.scalar.activation(out=gate[h][:], in_=og_raw[h][:], func=SIGMOID)
+
+        def gate_scale(h, b):
+            cols = slice(512 * b, 512 * (b + 1))
+            nc.vector.tensor_tensor(out=res[h][:, cols], in0=y_bank[h][:], in1=gate[h][:, cols], op=MULT)
+
+        def store(h):
+            nc.sync.dma_start(out=out[h].rearrange("(p r) e -> p (r e)", r=TILES), in_=res[h][:])
+
+        for g in range(PASSES):
+            key_factors(g)
+        for g in range(PASSES):
+            for h in range(H):
+                key_sigmoid(g, h)
+                key_scale(g, h)
+                if (g, h) == (1, 0):
+                    key_quantize(0)
+        key_quantize(1)
+
+        for a in range(HALVES):
+            for u in range(2):
+                query_sigmoid(a, u)
+        for r in range(TILES):
+            query_scale(0, r)
+        value_round(0, nc.scalar.copy)
+        for r in range(4):
+            query_scale(1, r)
+        value_quantize(0)
+        state_products(0)
+        value_round(1, nc.scalar.copy)
+        for r in range(4, TILES):
+            query_scale(1, r)
+        value_quantize(1)
+        state_products(1)
+        value_round(2, nc.vector.tensor_copy)
+        query_quantize(0)
+        value_quantize(2)
+        state_products(2)
+        value_round(3, nc.vector.tensor_copy)
+        query_quantize(1)
+        value_quantize(3)
+        state_products(3)
+        state_round(0)
+        state_round(1)
+        state_round(2)
+        gate_sigmoid(0)
+        state_round(3)
+        quantize(s_codes, s_scales, state[:].rearrange("p e x -> p (e x)"))
+        for h in range(1, H):
+            gate_sigmoid(h)
+        for h in range(H):
+            read_state(h, 0)
+        for pair in ((0, 1), (2, 3)):
+            for h in pair:
+                gate_scale(h, 0)
+                read_state(h, 1)
+            for h in pair:
+                gate_scale(h, 1)
+                store(h)

@@ -21,6 +21,7 @@ PASSES = N // (P * PACK)
 TILES = N // P
 HALVES = 2
 BANK_TILES = 4
+LEAD = 3
 
 
 def tile_rows_lin_sig_gate_kernel(tc, q, qa, ka, k, t, v, og, out):
@@ -53,10 +54,12 @@ def tile_rows_lin_sig_gate_kernel(tc, q, qa, ka, k, t, v, og, out):
         for a in range(HALVES):
             for u in range(2):
                 nc.sync.dma_start(out=q_raw[a][u][:], in_=q_rows[:, 2 * u : 2 * u + 2, 512 * a : 512 * (a + 1)])
-        for h in range(H):
-            nc.sync.dma_start(out=v_raw[h][:], in_=v[h].rearrange("(g p j) e -> p g j e", p=P, j=PACK))
-        for h in range(H):
-            nc.sync.dma_start(out=og_raw[h][:], in_=og[h].rearrange("(p r) e -> p (r e)", r=TILES))
+        for step in range(H + LEAD):
+            if step >= LEAD:
+                h = step - LEAD
+                nc.sync.dma_start(out=og_raw[h][:], in_=og[h].rearrange("(p r) e -> p (r e)", r=TILES))
+            if step < H:
+                nc.sync.dma_start(out=v_raw[step][:], in_=v[step].rearrange("(g p j) e -> p g j e", p=P, j=PACK))
 
         tka = [sbuf("tka%d" % g, [P, PACK, ROWS, PACK], F32) for g in range(PASSES)]
         k_sig = [[sbuf("k_sig%d%d" % (g, h), [P, PACK, ROWS, PACK], F32) for h in range(H)] for g in range(PASSES)]
@@ -71,12 +74,17 @@ def tile_rows_lin_sig_gate_kernel(tc, q, qa, ka, k, t, v, og, out):
         v_codes = [sbuf("v_codes%d" % h, [P, PASSES * D], U32) for h in range(H)]
         v_scales = [sbuf("v_scales%d" % h, [P, PASSES * D], U8) for h in range(H)]
         state = sbuf("state", [P, D, PACK], BF16)
-        s_codes = sbuf("s_codes", [P, D], U32)
-        s_scales = sbuf("s_scales", [P, D], U8)
+        s_codes = [sbuf("s_codes%d" % h, [P, D], U32) for h in range(H)]
+        s_scales = [sbuf("s_scales%d" % h, [P, D], U8) for h in range(H)]
         gate = [sbuf("gate%d" % h, [P, TILES * D], F32) for h in range(H)]
         res = [sbuf("res%d" % h, [P, TILES * D], F32) for h in range(H)]
-        s_bank = [ps.tile([P, PACK, D], F32, name="s_bank%d" % h) for h in range(H)]
-        y_bank = [ps.tile([P, BANK_TILES * D], F32, name="y_bank%d" % h) for h in range(H)]
+        s_banks = [ps.tile([P, PACK, D], F32, name="s_bank%d" % i) for i in range(2)]
+        s_bank = [s_banks[h % 2] for h in range(H)]
+        y_first = [ps.tile([P, BANK_TILES * D], F32, name="y_first%d" % h) for h in range(H)]
+        y_second = [
+            y_first[h] if h < 2 else ps.tile([P, BANK_TILES * D], F32, name="y_second%d" % h) for h in range(H)
+        ]
+        y_bank = [y_first, y_second]
 
         def quantize(codes, scales, values):
             nc.vector.quantize_mx(out=codes[:].bitcast(FP8X4), scales=scales[:], in_=values)
@@ -156,29 +164,39 @@ def tile_rows_lin_sig_gate_kernel(tc, q, qa, ka, k, t, v, og, out):
                 out=state[rows, :, :], in_=s_bank[h][rows, :, :].rearrange("p x e -> p e x"), func=COPY, scale=1.0 / N
             )
 
+        def state_quantize(h):
+            rows = slice(0, ROWS * (h + 1))
+            nc.vector.quantize_mx(
+                out=s_codes[h][rows, :].bitcast(FP8X4),
+                scales=s_scales[h][rows, :],
+                in_=state[rows, :, :].rearrange("p e x -> p (e x)"),
+            )
+
         def read_state(h, b):
             rows = slice(ROWS * h, ROWS * (h + 1))
             for i in range(BANK_TILES):
                 cols = slice(P * i, P * (i + 1))
                 nc.tensor.matmul_mx(
-                    out=y_bank[h][:, cols],
+                    out=y_bank[b][h][:, cols],
                     lhsT=q_codes[b][rows, cols].bitcast(FP8X4),
                     lhsT_scale=q_scales[b][rows, cols],
-                    rhs=s_codes[rows, :].bitcast(FP8X4),
-                    rhs_scale=s_scales[rows, :],
+                    rhs=s_codes[h][rows, :].bitcast(FP8X4),
+                    rhs_scale=s_scales[h][rows, :],
                     start=True,
                     stop=True,
                 )
 
-        def gate_sigmoid(h):
-            nc.scalar.activation(out=gate[h][:], in_=og_raw[h][:], func=SIGMOID)
+        def gate_sigmoid(h, b):
+            cols = slice(512 * b, 512 * (b + 1))
+            nc.scalar.activation(out=gate[h][:, cols], in_=og_raw[h][:, cols], func=SIGMOID)
 
         def gate_scale(h, b):
             cols = slice(512 * b, 512 * (b + 1))
-            nc.vector.tensor_tensor(out=res[h][:, cols], in0=y_bank[h][:], in1=gate[h][:, cols], op=MULT)
+            nc.vector.tensor_tensor(out=res[h][:, cols], in0=y_bank[b][h][:], in1=gate[h][:, cols], op=MULT)
 
-        def store(h):
-            nc.sync.dma_start(out=out[h].rearrange("(p r) e -> p (r e)", r=TILES), in_=res[h][:])
+        def store(h, b):
+            cols = slice(512 * b, 512 * (b + 1))
+            nc.sync.dma_start(out=out[h].rearrange("(p r) e -> p (r e)", r=TILES)[:, cols], in_=res[h][:, cols])
 
         for g in range(PASSES):
             key_factors(g)
@@ -190,43 +208,61 @@ def tile_rows_lin_sig_gate_kernel(tc, q, qa, ka, k, t, v, og, out):
                     key_quantize(0)
         key_quantize(1)
 
+        def finish(h, b):
+            gate_scale(h, b)
+            store(h, b)
+
         for a in range(HALVES):
             for u in range(2):
                 query_sigmoid(a, u)
         for r in range(TILES):
             query_scale(0, r)
-        value_round(0, nc.scalar.copy)
         for r in range(4):
             query_scale(1, r)
+        value_round(0, nc.scalar.copy)
         value_quantize(0)
         state_products(0)
-        value_round(1, nc.scalar.copy)
         for r in range(4, TILES):
             query_scale(1, r)
+        value_round(1, nc.scalar.copy)
         value_quantize(1)
         state_products(1)
-        value_round(2, nc.vector.tensor_copy)
         query_quantize(0)
+        value_round(2, nc.scalar.copy)
         value_quantize(2)
+        state_round(0)
         state_products(2)
-        value_round(3, nc.vector.tensor_copy)
         query_quantize(1)
+        state_quantize(0)
+        read_state(0, 0)
+        gate_sigmoid(0, 0)
+        value_round(3, nc.vector.tensor_copy)
+        state_round(1)
+        state_quantize(1)
+        read_state(1, 0)
         value_quantize(3)
         state_products(3)
-        state_round(0)
-        state_round(1)
+        gate_sigmoid(0, 1)
         state_round(2)
-        gate_sigmoid(0)
+        finish(0, 0)
+        state_quantize(2)
+        gate_sigmoid(1, 0)
+        finish(1, 0)
+        read_state(0, 1)
+        read_state(2, 0)
+        read_state(1, 1)
+        read_state(2, 1)
+        gate_sigmoid(2, 0)
         state_round(3)
-        quantize(s_codes, s_scales, state[:].rearrange("p e x -> p (e x)"))
-        for h in range(1, H):
-            gate_sigmoid(h)
-        for h in range(H):
-            read_state(h, 0)
-        for pair in ((0, 1), (2, 3)):
-            for h in pair:
-                gate_scale(h, 0)
-                read_state(h, 1)
-            for h in pair:
-                gate_scale(h, 1)
-                store(h)
+        finish(0, 1)
+        finish(2, 0)
+        state_quantize(3)
+        read_state(3, 0)
+        read_state(3, 1)
+        gate_sigmoid(1, 1)
+        finish(1, 1)
+        gate_sigmoid(2, 1)
+        finish(2, 1)
+        for b in range(2):
+            gate_sigmoid(3, b)
+            finish(3, b)

@@ -32,7 +32,7 @@ def tile_rows_lin_sig_gate_kernel(tc, q, qa, ka, k, t, v, og, out):
         ctx.enter_context(tc.manual_schedule())
 
         def sbuf(name, shape, dtype):
-            return sb.tile(shape, dtype, name=name, align_bytes=64)
+            return sb.tile(shape, dtype, name=name, align_bytes=256)
 
         ka_sb = sbuf("ka", [P, D], F32)
         t_sb = sbuf("t", [P, PASSES, PACK], F32)

from contextlib import ExitStack

import concourse.mybir as mybir

H, D, N = 4, 128, 1024
FLOPS = 2 * 2 * H * N * D * D

F32 = mybir.dt.float32
BF16 = mybir.dt.bfloat16
U32 = mybir.dt.uint32
U8 = mybir.dt.uint8
FP8X4 = mybir.dt.float8_e4m3fn_x4
SIGMOID = mybir.ActivationFunctionType.Sigmoid
COPY = mybir.ActivationFunctionType.Copy
MULT = mybir.AluOpType.mult

P = 128
PACK = 4
ROWS = D // PACK
PASSES = N // (P * PACK)
TILES = N // P
HALVES = 2
BANK_TILES = 4
LEAD = 3


def tile_rows_lin_sig_gate_kernel(tc, q, qa, ka, k, t, v, og, out):
    nc = tc.nc
    with ExitStack() as ctx:
        sb = ctx.enter_context(tc.tile_pool(name="sb", bufs=1))
        ps = ctx.enter_context(tc.psum_pool(name="ps", bufs=1))
        ctx.enter_context(tc.manual_schedule())

        def sbuf(name, shape, dtype):
            return sb.tile(shape, dtype, name=name, align_bytes=256)

        ka_sb = sbuf("ka", [P, D], F32)
        t_sb = sbuf("t", [P, PASSES, PACK], F32)
        qa_sb = sbuf("qa", [P, PACK], F32)
        k_raw = [[sbuf("k_raw%d%d" % (g, h), [P, PACK, D], F32) for h in range(H)] for g in range(PASSES)]
        q_raw = [[sbuf("q_raw%d%d" % (a, u), [P, 2, N // HALVES], F32) for u in range(2)] for a in range(HALVES)]
        v_raw = [sbuf("v_raw%d" % h, [P, PASSES, PACK, D], F32) for h in range(H)]
        og_raw = [sbuf("og_raw%d" % h, [P, TILES * D], F32) for h in range(H)]

        nc.sync.dma_start(out=ka_sb[:], in_=ka)
        nc.sync.dma_start(out=t_sb[:], in_=t.rearrange("(g p j) o -> p g (j o)", p=P, j=PACK))
        for g in range(PASSES):
            for h in range(H):
                nc.sync.dma_start(out=k_raw[g][h][:], in_=k[h].rearrange("(g p j) d -> g p j d", p=P, j=PACK)[g])
        nc.sync.dma_start(
            out=qa_sb[:], in_=qa.rearrange("(p j) o -> p (j o)", j=PACK).unsqueeze(0).to_broadcast([H, ROWS, PACK])
        )
        q_rows = q.rearrange("h (p j) n -> (h p) j n", j=PACK)
        for a in range(HALVES):
            for u in range(2):
                nc.sync.dma_start(out=q_raw[a][u][:], in_=q_rows[:, 2 * u : 2 * u + 2, 512 * a : 512 * (a + 1)])
        for step in range(H + LEAD):
            if step >= LEAD:
                h = step - LEAD
                nc.sync.dma_start(out=og_raw[h][:], in_=og[h].rearrange("(p r) e -> p (r e)", r=TILES))
            if step < H:
                nc.sync.dma_start(out=v_raw[step][:], in_=v[step].rearrange("(g p j) e -> p g j e", p=P, j=PACK))

        tka = [sbuf("tka%d" % g, [P, PACK, ROWS, PACK], F32) for g in range(PASSES)]
        k_sig = [[sbuf("k_sig%d%d" % (g, h), [P, PACK, ROWS, PACK], F32) for h in range(H)] for g in range(PASSES)]
        fk = [sbuf("fk%d" % g, [P, PACK, H, ROWS * PACK], BF16) for g in range(PASSES)]
        k_codes = [sbuf("k_codes%d" % g, [P, PACK * P], U32) for g in range(PASSES)]
        k_scales = [sbuf("k_scales%d" % g, [P, PACK * P], U8) for g in range(PASSES)]
        q_sig = [sbuf("q_sig%d" % a, [P, 2, N // HALVES, 2], F32) for a in range(HALVES)]
        fq = [sbuf("fq%d" % b, [P, BANK_TILES, P, PACK], BF16) for b in range(2)]
        q_codes = [sbuf("q_codes%d" % b, [P, BANK_TILES * P], U32) for b in range(2)]
        q_scales = [sbuf("q_scales%d" % b, [P, BANK_TILES * P], U8) for b in range(2)]
        vb = [sbuf("vb%d" % h, [P, PASSES, D, PACK], BF16) for h in range(H)]
        v_codes = [sbuf("v_codes%d" % h, [P, PASSES * D], U32) for h in range(H)]
        v_scales = [sbuf("v_scales%d" % h, [P, PASSES * D], U8) for h in range(H)]
        state = sbuf("state", [P, D, PACK], BF16)
        s_codes = [sbuf("s_codes%d" % h, [P, D], U32) for h in range(H)]
        s_scales = [sbuf("s_scales%d" % h, [P, D], U8) for h in range(H)]
        gate = [sbuf("gate%d" % h, [P, TILES * D], F32) for h in range(H)]
        res = [sbuf("res%d" % h, [P, TILES * D], F32) for h in range(H)]
        s_banks = [ps.tile([P, PACK, D], F32, name="s_bank%d" % i) for i in range(2)]
        s_bank = [s_banks[h % 2] for h in range(H)]
        y_first = [ps.tile([P, BANK_TILES * D], F32, name="y_first%d" % h) for h in range(H)]
        y_second = [
            y_first[h] if h < 2 else ps.tile([P, BANK_TILES * D], F32, name="y_second%d" % h) for h in range(H)
        ]
        y_bank = [y_first, y_second]

        def quantize(codes, scales, values):
            nc.vector.quantize_mx(out=codes[:].bitcast(FP8X4), scales=scales[:], in_=values)

        def key_factors(g):
            shape = [P, PACK, ROWS, PACK]
            nc.vector.tensor_tensor(
                out=tka[g][:],
                in0=ka_sb[:].rearrange("p (c x) -> p x c", x=PACK).unsqueeze(3).to_broadcast(shape),
                in1=t_sb[:, g, :].unsqueeze(1).unsqueeze(1).to_broadcast(shape),
                op=MULT,
            )

        def key_sigmoid(g, h):
            nc.scalar.activation(
                out=k_sig[g][h][:].rearrange("p x c j -> p c j x"),
                in_=k_raw[g][h][:].rearrange("p j (c x) -> p c j x", x=PACK),
                func=SIGMOID,
            )

        def key_scale(g, h):
            nc.vector.tensor_tensor(
                out=fk[g][:, :, h, :],
                in0=k_sig[g][h][:].rearrange("p x c j -> p x (c j)"),
                in1=tka[g][:].rearrange("p x c j -> p x (c j)"),
                op=MULT,
            )

        def key_quantize(g):
            quantize(k_codes[g], k_scales[g], fk[g][:].rearrange("p x h w -> p (x h w)"))

        def query_sigmoid(a, u):
            nc.scalar.activation(out=q_sig[a][:, u, :, :], in_=q_raw[a][u][:].rearrange("p e n -> p n e"), func=SIGMOID)

        def query_scale(a, r):
            width = P // HALVES
            shape = [P, width, 2, 2]
            nc.vector.tensor_tensor(
                out=fq[r // BANK_TILES][:, r % BANK_TILES, width * a : width * (a + 1), :].rearrange(
                    "p s (u e) -> p s u e", u=2
                ),
                in0=q_sig[a][:].rearrange("p u (s r) e -> p r s u e", r=TILES)[:, r],
                in1=qa_sb[:].rearrange("p (u e) -> p u e", u=2).unsqueeze(1).to_broadcast(shape),
                op=MULT,
            )

        def query_quantize(b):
            quantize(q_codes[b], q_scales[b], fq[b][:].rearrange("p r s j -> p (r s j)"))

        def value_round(h, copy):
            copy(
                out=vb[h][:].rearrange("p g (c i) j -> p g c j i", i=4),
                in_=v_raw[h][:].rearrange("p g j (c i) -> p g c j i", i=4),
            )

        def value_quantize(h):
            quantize(v_codes[h], v_scales[h], vb[h][:].rearrange("p g e j -> p (g e j)"))

        def state_products(h):
            for x in range(PACK):
                for g in range(PASSES):
                    k_cols = slice(P * x, P * (x + 1))
                    v_cols = slice(D * g, D * (g + 1))
                    nc.tensor.matmul_mx(
                        out=s_bank[h][:, x, :],
                        lhsT=k_codes[g][:, k_cols].bitcast(FP8X4),
                        lhsT_scale=k_scales[g][:, k_cols],
                        rhs=v_codes[h][:, v_cols].bitcast(FP8X4),
                        rhs_scale=v_scales[h][:, v_cols],
                        start=(g == 0),
                        stop=(g == PASSES - 1),
                    )

        def state_round(h):
            rows = slice(ROWS * h, ROWS * (h + 1))
            nc.scalar.activation(
                out=state[rows, :, :], in_=s_bank[h][rows, :, :].rearrange("p x e -> p e x"), func=COPY, scale=1.0 / N
            )

        def state_quantize(h):
            rows = slice(0, ROWS * (h + 1))
            nc.vector.quantize_mx(
                out=s_codes[h][rows, :].bitcast(FP8X4),
                scales=s_scales[h][rows, :],
                in_=state[rows, :, :].rearrange("p e x -> p (e x)"),
            )

        def read_state(h, b):
            rows = slice(ROWS * h, ROWS * (h + 1))
            for i in range(BANK_TILES):
                cols = slice(P * i, P * (i + 1))
                nc.tensor.matmul_mx(
                    out=y_bank[b][h][:, cols],
                    lhsT=q_codes[b][rows, cols].bitcast(FP8X4),
                    lhsT_scale=q_scales[b][rows, cols],
                    rhs=s_codes[h][rows, :].bitcast(FP8X4),
                    rhs_scale=s_scales[h][rows, :],
                    start=True,
                    stop=True,
                )

        def gate_sigmoid(h, b):
            cols = slice(512 * b, 512 * (b + 1))
            nc.scalar.activation(out=gate[h][:, cols], in_=og_raw[h][:, cols], func=SIGMOID)

        def gate_scale(h, b):
            cols = slice(512 * b, 512 * (b + 1))
            nc.vector.tensor_tensor(out=res[h][:, cols], in0=y_bank[b][h][:], in1=gate[h][:, cols], op=MULT)

        def store(h, b):
            cols = slice(512 * b, 512 * (b + 1))
            nc.sync.dma_start(out=out[h].rearrange("(p r) e -> p (r e)", r=TILES)[:, cols], in_=res[h][:, cols])

        for g in range(PASSES):
            key_factors(g)
        for g in range(PASSES):
            for h in range(H):
                key_sigmoid(g, h)
                key_scale(g, h)
                if (g, h) == (1, 0):
                    key_quantize(0)
        key_quantize(1)

        def finish(h, b):
            gate_scale(h, b)
            store(h, b)

        for a in range(HALVES):
            for u in range(2):
                query_sigmoid(a, u)
        for r in range(TILES):
            query_scale(0, r)
        for r in range(4):
            query_scale(1, r)
        value_round(0, nc.scalar.copy)
        value_quantize(0)
        state_products(0)
        for r in range(4, TILES):
            query_scale(1, r)
        value_round(1, nc.scalar.copy)
        value_quantize(1)
        state_products(1)
        query_quantize(0)
        value_round(2, nc.scalar.copy)
        value_quantize(2)
        state_round(0)
        state_products(2)
        query_quantize(1)
        state_quantize(0)
        read_state(0, 0)
        gate_sigmoid(0, 0)
        value_round(3, nc.vector.tensor_copy)
        state_round(1)
        state_quantize(1)
        read_state(1, 0)
        value_quantize(3)
        state_products(3)
        gate_sigmoid(0, 1)
        state_round(2)
        finish(0, 0)
        state_quantize(2)
        gate_sigmoid(1, 0)
        finish(1, 0)
        read_state(0, 1)
        read_state(2, 0)
        read_state(1, 1)
        read_state(2, 1)
        gate_sigmoid(2, 0)
        state_round(3)
        finish(0, 1)
        finish(2, 0)
        state_quantize(3)
        read_state(3, 0)
        read_state(3, 1)
        gate_sigmoid(1, 1)
        finish(1, 1)
        gate_sigmoid(2, 1)
        finish(2, 1)
        for b in range(2):
            gate_sigmoid(3, b)
            finish(3, b)
